import numpy as np
import ml_dtypes


def mxq(x, axis, fmt="e4m3"):
    dtype, down = {"e4m3": (ml_dtypes.float8_e4m3fn, 7), "e5m2": (ml_dtypes.float8_e5m2, 14)}[fmt]
    v = np.moveaxis(np.asarray(x, np.float32).astype(ml_dtypes.bfloat16).astype(np.float64), axis, -1)
    blocks = v.reshape(v.shape[:-1] + (-1, 32))
    amax = np.abs(blocks).max(-1, keepdims=True)
    byte = np.maximum(np.where(amax > 0, np.frexp(amax)[1] - 1 + 127, 0) - down, 1)
    scale = np.exp2(byte - 127.0)
    codes = (blocks / scale).astype(np.float32).astype(dtype).astype(np.float64)
    return np.moveaxis((codes * scale).reshape(v.shape), -1, axis)


WIDE = False


def mx_kscale(k):
    if not WIDE:
        return np.ones(k)
    levels = np.array([10, -10, 5, -5, 0])
    if k % 512:
        return np.exp2(np.random.permutation(np.resize(levels, k // 32))).repeat(32)
    a = np.empty((k // 512, 16))
    for p in range(k // 512):
        a[p, :8] = np.random.permutation(np.resize(levels, 8))
        for g in range(8):
            far = levels[np.abs(levels - a[p, g]) >= 10]
            a[p, g + 8] = far[np.random.randint(len(far))]
    return np.exp2(a.ravel()).repeat(32)


def f64(x):
    return np.asarray(x).astype(np.float64)


def striped(idx):
    return np.tile(idx.reshape(-1, 16).T, (8, 1)).astype(np.uint16)


def unstriped(offs):
    return offs[:16].T.reshape(-1).astype(np.int64)


def gelu(v):
    return 0.5 * v * (1.0 + np.tanh(np.sqrt(2.0 / np.pi) * (v + 0.044715 * v**3)))


K, T, E, C, H, N = 512, 512, 12, 128, 512, 128
TOP = 3


def by_expert(wq, xq):
    return np.concatenate([wq[e].T @ xq[:, e * C:(e + 1) * C] for e in range(E)], axis=1)


def setup_inputs():
    n = np.random.standard_normal
    s = mx_kscale(K)[:, None]
    u = mx_kscale(H)
    deal = np.repeat(np.arange(E), C).reshape(TOP, T)[:, np.random.permutation(T)]
    deal = np.take_along_axis(deal, np.argsort(np.random.rand(TOP, T), axis=0), axis=0)
    for _ in range(8):
        s_, t_ = np.random.permutation(T).reshape(2, -1); r = np.random.randint(TOP, size=T // 2); x, y = deal[r, s_].copy(), deal[r, t_].copy()
        ok = ~((deal[:, s_] == y).any(0) | (deal[:, t_] == x).any(0)); deal[r[ok], s_[ok]] = y[ok]; deal[r[ok], t_[ok]] = x[ok]
    order = np.lexsort((np.random.rand(TOP * T), deal.reshape(-1)))
    slot_token = order % T; pos = np.empty(TOP * T, np.int64); pos[order] = np.arange(TOP * T); pos = pos.reshape(TOP, T)
    g = np.random.uniform(0.5, 1.5, (TOP, T)); g = g / g.sum(0)
    return {
        "xT": (n((K, T)) * s).astype(np.float32),
        "w1": (n((E, K, H)) / np.sqrt(K) / s[None]).astype(np.float32),
        "w3": (n((E, K, H)) / np.sqrt(K) / s[None] * u[None, None, :]).astype(np.float32),
        "w2": (n((E, H, N)) / np.sqrt(H) / u[None, :, None]).astype(np.float32),
        "gate": np.stack([np.tile(r, (N, 1)) for r in g]).astype(np.float32),
        "offs": striped(slot_token),
        "pos1": striped(pos[0]),
        "pos2": striped(pos[1]),
        "pos3": striped(pos[2]),
    }


def reference(xT, w1, w3, w2, gate, offs, pos1, pos2, pos3):
    idx = unstriped(offs)
    xq = mxq(f64(xT)[:, idx], 0, "e4m3")
    h = gelu(by_expert(mxq(f64(w1), 1, "e4m3"), xq))
    h = h * by_expert(mxq(f64(w3), 1, "e4m3"), xq)
    y = by_expert(mxq(f64(w2), 1, "e4m3"), mxq(h, 0, "e4m3"))
    return sum(f64(gate[r]) * y[:, unstriped(p)] for r, p in enumerate((pos1, pos2, pos3)))

@@ -1,0 +1,247 @@
+from contextlib import ExitStack
+
+import concourse.mybir as mybir
+
+K, T, E, C, H, N = 512, 512, 12, 128, 512, 128
+FLOPS = 2 * E * C * (2 * K * H + H * N)
+
+P = 128
+F32 = mybir.dt.float32
+BF16 = mybir.dt.bfloat16
+U32 = mybir.dt.uint32
+U16 = mybir.dt.uint16
+U8 = mybir.dt.uint8
+FP8X4 = mybir.dt.float8_e4m3fn_x4
+MULT = mybir.AluOpType.mult
+ADD = mybir.AluOpType.add
+GELU = mybir.ActivationFunctionType.Gelu_apprx_tanh
+
+W2_GROUPS = ((0, 4), (4, 4), (8, 2), (10, 2))
+GATHERS = ((0, 128), (128, 256), (384, 384), (768, 384), (1152, 384))
+
+
+def tile_moe_tk_glu_gelu_kernel(tc, xT, w1, w3, w2, gate, offs, pos1, pos2, pos3, out):
+    nc = tc.nc
+    with ExitStack() as ctx:
+        keep = ctx.enter_context(tc.tile_pool(name="keep", bufs=1))
+        raws = ctx.enter_context(tc.tile_pool(name="raws", bufs=8))
+        raw2s = ctx.enter_context(tc.tile_pool(name="raw2s", bufs=2))
+        rounds = ctx.enter_context(tc.tile_pool(name="rounds", bufs=2))
+        codes_pool = ctx.enter_context(tc.tile_pool(name="codes", bufs=3))
+        h_codes_pool = ctx.enter_context(tc.tile_pool(name="h_codes", bufs=6))
+        hidden = ctx.enter_context(tc.tile_pool(name="hidden", bufs=2))
+        psum = ctx.enter_context(tc.psum_pool(name="psum", bufs=3))
+        psum_y = ctx.enter_context(tc.psum_pool(name="psum_y", bufs=2))
+
+        offs_t = keep.tile([P, E * C // 16], U16, name="offs_t")
+        pos_t = [keep.tile([P, T // 16], U16, name=f"pos_t{r}") for r in range(3)]
+        gate_t = keep.tile([P, 3, T], F32, name="gate_t")
+        x_raw = keep.tile([P, 4, T], F32, name="x_raw")
+        x_bf = keep.tile([P, T, 4], BF16, align_bytes=64, name="x_bf")
+        x_codes = keep.tile([P, T], U32, align_bytes=64, name="x_codes")
+        x_scales = keep.tile([P, T], U8, align_bytes=64, name="x_scales")
+        g_codes = keep.tile([P, E * C], U32, align_bytes=64, name="g_codes")
+        g_scales = keep.tile([P, E * C], U8, align_bytes=64, name="g_scales")
+        y_all = keep.tile([P, E * C], F32, name="y_all")
+        prods = keep.tile([P, 3, T], F32, name="prods")
+        part = keep.tile([P, T], F32, name="part")
+        result = keep.tile([P, T], F32, name="result")
+        warm = keep.tile([P, 8], F32, name="warm")
+
+        nc.gpsimd.memset(x_scales[:], 0)
+        nc.vector.memset(warm[:], 0.0)
+        nc.scalar.activation(warm[:], warm[:], GELU)
+
+        nc.sync.dma_start(x_raw[:], xT.rearrange("(p j) t -> p j t", j=4))
+        nc.sync.dma_start(offs_t[:], offs)
+
+        raw1 = {}
+        raw3 = {}
+        raw2 = {}
+
+        def load13(e):
+            raw1[e] = raws.tile([P, 4, H], F32, name="raw1", tag="raw")
+            nc.sync.dma_start(raw1[e][:], w1[e].rearrange("(p j) i -> p j i", j=4))
+            raw3[e] = raws.tile([P, 4, H], F32, name="raw3", tag="raw")
+            nc.sync.dma_start(raw3[e][:], w3[e].rearrange("(p j) i -> p j i", j=4))
+
+        def load2(first, count):
+            tile = raw2s.tile([P, count, 4, N], F32, name=f"raw2_{count}")
+            nc.sync.dma_start(tile[:], w2[first : first + count].rearrange("e (p j) n -> p e j n", j=4))
+            for e in range(first, first + count):
+                raw2[e] = (tile, e - first)
+
+        def interleave_hidden(engine_copy, dst, src, m0, m1):
+            engine_copy(
+                dst[:].rearrange("p (t m j) -> p m j t", t=4, j=4)[:, m0:m1],
+                src[:].rearrange("p j (m t) -> p m j t", t=4)[:, m0:m1],
+            )
+
+        def interleave(engine_copy, dst, src):
+            engine_copy(
+                dst.rearrange("p (c i j) -> p c j i", i=4, j=4),
+                src.rearrange("p j (c i) -> p c j i", i=4),
+            )
+
+        split = 320
+        xb = x_bf[:].rearrange("p t j -> p (t j)")
+        interleave(nc.vector.tensor_copy, xb[:, : 4 * split], x_raw[:, :, :split])
+        interleave(nc.scalar.copy, xb[:, 4 * split :], x_raw[:, :, split:])
+        nc.vector.quantize_mx(out=x_codes[:].bitcast(FP8X4), scales=x_scales[:], in_=xb)
+
+        def gather(i):
+            s, n = GATHERS[i]
+            lists = offs_t[:, s // 16 : (s + n) // 16]
+            nc.vector.tensor_copy(g_codes[:, s : s + n], x_codes[:].indirect(lists))
+            nc.vector.tensor_copy(g_scales[:, s : s + n], x_scales[:].indirect(lists))
+
+        bf1 = {}
+        bf3 = {}
+        q1 = {}
+        q3 = {}
+        q2 = {}
+        act = {}
+        acc_b = {}
+        hb = {}
+        y_banks = {}
+        qh = {}
+
+        def quantise(src, width, tag):
+            pool = h_codes_pool if tag == "h" else codes_pool
+            codes = pool.tile([P, width], U32, align_bytes=64, name=f"codes_{tag}")
+            scales = pool.tile([P, width], U8, align_bytes=64, name=f"scales_{tag}")
+            nc.vector.quantize_mx(out=codes[:].bitcast(FP8X4), scales=scales[:], in_=src[:])
+            return codes, scales
+
+        def product(bank, q, e):
+            codes, scales = q
+            for t in range(4):
+                nc.tensor.matmul_mx(
+                    out=bank[:, t, :],
+                    lhsT=codes[:, t * P : (t + 1) * P].bitcast(FP8X4),
+                    lhsT_scale=scales[:, t * P : (t + 1) * P],
+                    rhs=g_codes[:, e * C : (e + 1) * C].bitcast(FP8X4),
+                    rhs_scale=g_scales[:, e * C : (e + 1) * C],
+                    start=True,
+                    stop=True,
+                )
+
+        def stage_gelu(e):
+            act[e] = hidden.tile([P, C, 4], F32, name="act")
+            bank = acc_a[e]
+            nc.scalar.activation(act[e][:], bank[:].rearrange("p t n -> p n t"), GELU)
+
+        acc_a = {}
+
+        def stage_a(e):
+            acc_a[e] = psum.tile([P, 4, C], F32, name="acc_a")
+            product(acc_a[e], q1[e], e)
+
+        def stage_b(e):
+            acc_b[e] = psum.tile([P, 4, C], F32, name="acc_b")
+            product(acc_b[e], q3[e], e)
+
+        def stage_mult(e):
+            hb[e] = hidden.tile([P, C * 4], BF16, align_bytes=64, name="hb")
+            nc.vector.tensor_tensor(
+                hb[e][:].rearrange("p (n t) -> p n t", t=4), act[e][:], acc_b[e][:].rearrange("p t n -> p n t"), MULT
+            )
+
+        def stage_h(e):
+            qh[e] = quantise(hb[e], C, "h")
+
+        def stage_y(e):
+            h_codes, h_scales = qh[e]
+            g = e // 4
+            if e % 4 == 0:
+                y_banks[g] = psum_y.tile([P, 4, C], F32, name="y_bank")
+            codes, scales, at = q2[e]
+            nc.tensor.matmul_mx(
+                out=y_banks[g][:, e % 4, :],
+                lhsT=codes[:, at : at + N].bitcast(FP8X4),
+                lhsT_scale=scales[:, at : at + N],
+                rhs=h_codes[:].bitcast(FP8X4),
+                rhs_scale=h_scales[:],
+                start=True,
+                stop=True,
+            )
+
+        def y_out(first, count):
+            nc.scalar.copy(
+                y_all[:, first * C : (first + count) * C],
+                y_banks[first // 4][:, first % 4 : first % 4 + count, :].rearrange("p e n -> p (e n)"),
+            )
+
+        def prepare_w2(first, count):
+            bf = rounds.tile([P, count * 4 * N], BF16, align_bytes=64, name=f"bf2_{count}")
+            for i in range(count):
+                tile, at = raw2[first + i]
+                interleave(nc.scalar.copy, bf[:, i * 4 * N : (i + 1) * 4 * N], tile[:, at])
+            return bf
+
+        def quantise_w2(bf, first, count):
+            codes, scales = quantise(bf, count * N, f"w2_{count}")
+            for i in range(count):
+                q2[first + i] = (codes, scales, i * N)
+
+        load13(0)
+        load2(0, 4)
+        load13(1)
+        for r, p in enumerate((pos1, pos2, pos3)):
+            nc.sync.dma_start(pos_t[r][:], p)
+        for e in range(2, E):
+            load13(e)
+            if e == 3:
+                load2(4, 4)
+        load2(8, 2)
+        load2(10, 2)
+        for r in range(3):
+            nc.sync.dma_start(gate_t[:, r, :], gate[r])
+
+        gather(0)
+        bf2 = {}
+        for e in range(E + 1):
+            if e >= 1:
+                stage_gelu(e - 1)
+                q3[e - 1] = quantise(bf3[e - 1], H, "w3")
+                stage_b(e - 1)
+            if e < E:
+                bf1[e] = rounds.tile([P, 4 * H], BF16, align_bytes=64, name="bf1")
+                interleave_hidden(nc.vector.tensor_copy, bf1[e], raw1[e], 0, P)
+                bf3[e] = rounds.tile([P, 4 * H], BF16, align_bytes=64, name="bf3")
+                interleave_hidden(nc.scalar.copy, bf3[e], raw3[e], 0, P)
+            if 1 <= e < 5:
+                gather(e)
+            if e >= 1:
+                stage_mult(e - 1)
+            if e < E:
+                q1[e] = quantise(bf1[e], H, "w1")
+                stage_a(e)
+            for first, count in W2_GROUPS:
+                if e == (E if first >= 8 else first + 1):
+                    bf2[first] = prepare_w2(first, count)
+            if e >= 1:
+                stage_h(e - 1)
+            for first, count in W2_GROUPS:
+                if e == (E if first >= 8 else first + 1):
+                    quantise_w2(bf2[first], first, count)
+            if 1 <= e <= 8:
+                stage_y(e - 1)
+                if e % 4 == 0:
+                    y_out(e - 4, 4)
+        for first, count in W2_GROUPS[2:]:
+            for i in range(count):
+                stage_y(first + i)
+            y_out(first, count)
+
+        halves = ((0, 256), (256, 256))
+        for r in range(3):
+            for s, n in halves:
+                nc.vector.tensor_tensor(
+                    prods[:, r, s : s + n], y_all[:].indirect(pos_t[r][:, s // 16 : (s + n) // 16]), gate_t[:, r, s : s + n], MULT
+                )
+        for s, n in halves:
+            nc.vector.tensor_tensor(part[:, s : s + n], prods[:, 0, s : s + n], prods[:, 1, s : s + n], ADD)
+        for s, n in halves:
+            nc.vector.tensor_tensor(result[:, s : s + n], part[:, s : s + n], prods[:, 2, s : s + n], ADD)
+            nc.sync.dma_start(out[:, s : s + n], result[:, s : s + n])

@@ -17,25 +17,23 @@ ADD = mybir.AluOpType.add
 GELU = mybir.ActivationFunctionType.Gelu_apprx_tanh
 
 W2_GROUPS = ((0, 4), (4, 4), (8, 2), (10, 2))
-GATHERS = ((0, 128), (128, 256), (384, 384), (768, 384), (1152, 384))
+GATHERS = ((0, 384), (384, 384), (768, 384), (1152, 384))
 
 
 def tile_moe_tk_glu_gelu_kernel(tc, xT, w1, w3, w2, gate, offs, pos1, pos2, pos3, out):
     nc = tc.nc
     with ExitStack() as ctx:
         keep = ctx.enter_context(tc.tile_pool(name="keep", bufs=1))
-        raws = ctx.enter_context(tc.tile_pool(name="raws", bufs=8))
-        raw2s = ctx.enter_context(tc.tile_pool(name="raw2s", bufs=2))
-        rounds = ctx.enter_context(tc.tile_pool(name="rounds", bufs=2))
+        raws = ctx.enter_context(tc.tile_pool(name="raws", bufs=6))
+        rounds = ctx.enter_context(tc.tile_pool(name="rounds", bufs=3))
         codes_pool = ctx.enter_context(tc.tile_pool(name="codes", bufs=3))
-        h_codes_pool = ctx.enter_context(tc.tile_pool(name="h_codes", bufs=6))
-        hidden = ctx.enter_context(tc.tile_pool(name="hidden", bufs=2))
+        h_pool = ctx.enter_context(tc.tile_pool(name="h_codes", bufs=12))
+        hidden = ctx.enter_context(tc.tile_pool(name="hidden", bufs=3))
         psum = ctx.enter_context(tc.psum_pool(name="psum", bufs=3))
         psum_y = ctx.enter_context(tc.psum_pool(name="psum_y", bufs=2))
 
         offs_t = keep.tile([P, E * C // 16], U16, name="offs_t")
         pos_t = [keep.tile([P, T // 16], U16, name=f"pos_t{r}") for r in range(3)]
-        gate_t = keep.tile([P, 3, T], F32, name="gate_t")
         x_raw = keep.tile([P, 4, T], F32, name="x_raw")
         x_bf = keep.tile([P, T, 4], BF16, align_bytes=64, name="x_bf")
         x_codes = keep.tile([P, T], U32, align_bytes=64, name="x_codes")
@@ -59,22 +57,16 @@ def tile_moe_tk_glu_gelu_kernel(tc, xT, w1, w3, w2, gate, offs, pos1, pos2, pos3
         raw3 = {}
         raw2 = {}
 
-        def load13(e):
-            raw1[e] = raws.tile([P, 4, H], F32, name="raw1", tag="raw")
-            nc.sync.dma_start(raw1[e][:], w1[e].rearrange("(p j) i -> p j i", j=4))
-            raw3[e] = raws.tile([P, 4, H], F32, name="raw3", tag="raw")
-            nc.sync.dma_start(raw3[e][:], w3[e].rearrange("(p j) i -> p j i", j=4))
+        def load(where, source, first, count):
+            tile = raws.tile([P, count, 4, source.shape[2]], F32, name="raw", tag="raw")
+            nc.sync.dma_start(tile[:], source[first : first + count].rearrange("e (p j) i -> p e j i", j=4))
+            for i in range(count):
+                where[first + i] = tile[:, i]
 
-        def load2(first, count):
-            tile = raw2s.tile([P, count, 4, N], F32, name=f"raw2_{count}")
-            nc.sync.dma_start(tile[:], w2[first : first + count].rearrange("e (p j) n -> p e j n", j=4))
-            for e in range(first, first + count):
-                raw2[e] = (tile, e - first)
-
-        def interleave_hidden(engine_copy, dst, src, m0, m1):
+        def interleave_hidden(engine_copy, dst, src, t0, t1):
             engine_copy(
-                dst[:].rearrange("p (t m j) -> p m j t", t=4, j=4)[:, m0:m1],
-                src[:].rearrange("p j (m t) -> p m j t", t=4)[:, m0:m1],
+                dst.rearrange("p (t m j) -> p m j t", t=4, j=4)[:, :, :, t0:t1],
+                src.rearrange("p j (m t) -> p m j t", t=4)[:, :, :, t0:t1],
             )
 
         def interleave(engine_copy, dst, src):
@@ -83,55 +75,66 @@ def tile_moe_tk_glu_gelu_kernel(tc, xT, w1, w3, w2, gate, offs, pos1, pos2, pos3
                 src.rearrange("p j (c i) -> p c j i", i=4),
             )
 
+        vcopy, scopy = nc.vector.tensor_copy, nc.scalar.copy
+
+        for e in range(0, E, 2):
+            load(raw3, w3, e, 2)
+            if e in ():
+                load(raw1, w1, e, 1)
+                load(raw1, w1, e + 1, 1)
+            else:
+                load(raw1, w1, e, 2)
+            if e == 4:
+                for tile, source in zip(pos_t, (pos1, pos2, pos3)):
+                    nc.sync.dma_start(tile[:], source)
+        for first, count in W2_GROUPS[0:]:
+            load(raw2, w2, first, count)
+        gate_t = []
+        for r in range(3):
+            tile = raws.tile([P, T], F32, name="gate_tile", tag="raw")
+            gate_t.append(tile)
+            nc.sync.dma_start(tile[:], gate[r])
+
         split = 320
         xb = x_bf[:].rearrange("p t j -> p (t j)")
-        interleave(nc.vector.tensor_copy, xb[:, : 4 * split], x_raw[:, :, :split])
-        interleave(nc.scalar.copy, xb[:, 4 * split :], x_raw[:, :, split:])
+        interleave(vcopy, xb[:, : 4 * split], x_raw[:, :, :split])
+        interleave(scopy, xb[:, 4 * split :], x_raw[:, :, split:])
         nc.vector.quantize_mx(out=x_codes[:].bitcast(FP8X4), scales=x_scales[:], in_=xb)
-
-        def gather(i):
-            s, n = GATHERS[i]
+        for s, n in GATHERS:
             lists = offs_t[:, s // 16 : (s + n) // 16]
             nc.vector.tensor_copy(g_codes[:, s : s + n], x_codes[:].indirect(lists))
             nc.vector.tensor_copy(g_scales[:, s : s + n], x_scales[:].indirect(lists))
 
-        bf1 = {}
-        bf3 = {}
         q1 = {}
         q3 = {}
         q2 = {}
-        act = {}
+        qh = {}
+        acc_a = {}
         acc_b = {}
+        act = {}
         hb = {}
         y_banks = {}
-        qh = {}
 
-        def quantise(src, width, tag):
-            pool = h_codes_pool if tag == "h" else codes_pool
+        def quantise(src, tag, pool=codes_pool):
+            width = src.shape[1] // 4
             codes = pool.tile([P, width], U32, align_bytes=64, name=f"codes_{tag}")
             scales = pool.tile([P, width], U8, align_bytes=64, name=f"scales_{tag}")
-            nc.vector.quantize_mx(out=codes[:].bitcast(FP8X4), scales=scales[:], in_=src[:])
+            nc.vector.quantize_mx(out=codes[:].bitcast(FP8X4), scales=scales[:], in_=src)
             return codes, scales
 
         def product(bank, q, e):
-            codes, scales = q
+            codes, scales, at = q
             for t in range(4):
+                cols = slice(at + t * P, at + (t + 1) * P)
                 nc.tensor.matmul_mx(
                     out=bank[:, t, :],
-                    lhsT=codes[:, t * P : (t + 1) * P].bitcast(FP8X4),
-                    lhsT_scale=scales[:, t * P : (t + 1) * P],
+                    lhsT=codes[:, cols].bitcast(FP8X4),
+                    lhsT_scale=scales[:, cols],
                     rhs=g_codes[:, e * C : (e + 1) * C].bitcast(FP8X4),
                     rhs_scale=g_scales[:, e * C : (e + 1) * C],
                     start=True,
                     stop=True,
                 )
-
-        def stage_gelu(e):
-            act[e] = hidden.tile([P, C, 4], F32, name="act")
-            bank = acc_a[e]
-            nc.scalar.activation(act[e][:], bank[:].rearrange("p t n -> p n t"), GELU)
-
-        acc_a = {}
 
         def stage_a(e):
             acc_a[e] = psum.tile([P, 4, C], F32, name="acc_a")
@@ -141,6 +144,10 @@ def tile_moe_tk_glu_gelu_kernel(tc, xT, w1, w3, w2, gate, offs, pos1, pos2, pos3
             acc_b[e] = psum.tile([P, 4, C], F32, name="acc_b")
             product(acc_b[e], q3[e], e)
 
+        def stage_gelu(e):
+            act[e] = hidden.tile([P, C, 4], F32, name="act")
+            nc.scalar.activation(act[e][:], acc_a[e][:].rearrange("p t n -> p n t"), GELU)
+
         def stage_mult(e):
             hb[e] = hidden.tile([P, C * 4], BF16, align_bytes=64, name="hb")
             nc.vector.tensor_tensor(
@@ -148,7 +155,7 @@ def tile_moe_tk_glu_gelu_kernel(tc, xT, w1, w3, w2, gate, offs, pos1, pos2, pos3
             )
 
         def stage_h(e):
-            qh[e] = quantise(hb[e], C, "h")
+            qh[e] = quantise(hb[e][:], "h", h_pool)
 
         def stage_y(e):
             h_codes, h_scales = qh[e]
@@ -166,82 +173,66 @@ def tile_moe_tk_glu_gelu_kernel(tc, xT, w1, w3, w2, gate, offs, pos1, pos2, pos3
                 stop=True,
             )
 
-        def y_out(first, count):
-            nc.scalar.copy(
+        def y_out(first, count, copy):
+            copy(
                 y_all[:, first * C : (first + count) * C],
                 y_banks[first // 4][:, first % 4 : first % 4 + count, :].rearrange("p e n -> p (e n)"),
             )
 
-        def prepare_w2(first, count):
-            bf = rounds.tile([P, count * 4 * N], BF16, align_bytes=64, name=f"bf2_{count}")
-            for i in range(count):
-                tile, at = raw2[first + i]
-                interleave(nc.scalar.copy, bf[:, i * 4 * N : (i + 1) * 4 * N], tile[:, at])
+        def copy_w2(engines, first):
+            bf = rounds.tile([P, len(engines) * 4 * N], BF16, align_bytes=64, name="bf2")
+            for i, engine in enumerate(engines):
+                interleave(engine, bf[:, i * 4 * N : (i + 1) * 4 * N], raw2[first + i])
             return bf
 
-        def quantise_w2(bf, first, count):
-            codes, scales = quantise(bf, count * N, f"w2_{count}")
-            for i in range(count):
+        def quantise_w2(src, first):
+            codes, scales = quantise(src, "w2")
+            for i in range(src.shape[1] // (4 * N)):
                 q2[first + i] = (codes, scales, i * N)
 
-        load13(0)
-        load2(0, 4)
-        load13(1)
-        for r, p in enumerate((pos1, pos2, pos3)):
-            nc.sync.dma_start(pos_t[r][:], p)
-        for e in range(2, E):
-            load13(e)
-            if e == 3:
-                load2(4, 4)
-        load2(8, 2)
-        load2(10, 2)
-        for r in range(3):
-            nc.sync.dma_start(gate_t[:, r, :], gate[r])
+        def finish(group):
+            first, count = W2_GROUPS[group]
+            engines = ((scopy, vcopy, scopy, vcopy), (scopy, vcopy, scopy, vcopy), (scopy, vcopy), (scopy, vcopy))[group]
+            bf2 = copy_w2(engines, first)
+            quantise_w2(bf2[:], first)
+            for e in range(first, first + count):
+                stage_y(e)
+            y_out(first, count, vcopy if first == 10 else scopy)
 
-        gather(0)
-        bf2 = {}
-        for e in range(E + 1):
-            if e >= 1:
-                stage_gelu(e - 1)
-                q3[e - 1] = quantise(bf3[e - 1], H, "w3")
-                stage_b(e - 1)
-            if e < E:
-                bf1[e] = rounds.tile([P, 4 * H], BF16, align_bytes=64, name="bf1")
-                interleave_hidden(nc.vector.tensor_copy, bf1[e], raw1[e], 0, P)
-                bf3[e] = rounds.tile([P, 4 * H], BF16, align_bytes=64, name="bf3")
-                interleave_hidden(nc.scalar.copy, bf3[e], raw3[e], 0, P)
-            if 1 <= e < 5:
-                gather(e)
-            if e >= 1:
-                stage_mult(e - 1)
-            if e < E:
-                q1[e] = quantise(bf1[e], H, "w1")
+        for a in range(0, E, 2):
+            bf = {}
+            for e in (a, a + 1):
+                bf[e] = rounds.tile([P, 8 * H], BF16, align_bytes=64, name="bf")
+            for e, share in ((a, 0), (a + 1, 0)):
+                if share:
+                    interleave_hidden(vcopy, bf[e][:, 4 * H :], raw3[e], 0, share)
+                interleave_hidden(scopy, bf[e][:, 4 * H :], raw3[e], share, 4)
+            for e, share in ((a, 4 if a == E - 2 else 4), (a + 1, 4 if a == E - 2 else 4)):
+                interleave_hidden(vcopy, bf[e][:, : 4 * H], raw1[e], 0, share)
+                if share < 4:
+                    interleave_hidden(scopy, bf[e][:, : 4 * H], raw1[e], share, 4)
+            for e in (a, a + 1):
+                codes, scales = quantise(bf[e][:], "w")
+                q1[e] = (codes, scales, 0)
+                q3[e] = (codes, scales, H)
                 stage_a(e)
-            for first, count in W2_GROUPS:
-                if e == (E if first >= 8 else first + 1):
-                    bf2[first] = prepare_w2(first, count)
-            if e >= 1:
-                stage_h(e - 1)
-            for first, count in W2_GROUPS:
-                if e == (E if first >= 8 else first + 1):
-                    quantise_w2(bf2[first], first, count)
-            if 1 <= e <= 8:
-                stage_y(e - 1)
-                if e % 4 == 0:
-                    y_out(e - 4, 4)
-        for first, count in W2_GROUPS[2:]:
-            for i in range(count):
-                stage_y(first + i)
-            y_out(first, count)
+                stage_gelu(e)
+                stage_b(e)
+            for e in (a, a + 1):
+                stage_mult(e)
+            for e in (a, a + 1):
+                stage_h(e)
+        for group in range(0, len(W2_GROUPS)):
+            finish(group)
 
+        for r in range(2):
+            nc.vector.tensor_tensor(prods[:, r, :], y_all[:].indirect(pos_t[r][:]), gate_t[r][:], MULT)
         halves = ((0, 256), (256, 256))
-        for r in range(3):
-            for s, n in halves:
-                nc.vector.tensor_tensor(
-                    prods[:, r, s : s + n], y_all[:].indirect(pos_t[r][:, s // 16 : (s + n) // 16]), gate_t[:, r, s : s + n], MULT
-                )
-        for s, n in halves:
-            nc.vector.tensor_tensor(part[:, s : s + n], prods[:, 0, s : s + n], prods[:, 1, s : s + n], ADD)
-        for s, n in halves:
+        for i, (s, n) in enumerate(halves):
+            nc.vector.tensor_tensor(
+                prods[:, 2, s : s + n], y_all[:].indirect(pos_t[2][:, s // 16 : (s + n) // 16]), gate_t[2][:, s : s + n], MULT
+            )
+            if i == 0:
+                nc.vector.tensor_tensor(part[:], prods[:, 0, :], prods[:, 1, :], ADD)
             nc.vector.tensor_tensor(result[:, s : s + n], part[:, s : s + n], prods[:, 2, s : s + n], ADD)
             nc.sync.dma_start(out[:, s : s + n], result[:, s : s + n])

@@ -16,7 +16,7 @@ MULT = mybir.AluOpType.mult
 ADD = mybir.AluOpType.add
 GELU = mybir.ActivationFunctionType.Gelu_apprx_tanh
 
-W2_GROUPS = ((0, 4), (4, 4), (8, 2), (10, 2))
+PLAN = {'dma': [('3', 0, 2), ('1', 0, 1), ('1', 1, 1), ('3', 2, 2), ('1', 2, 1), ('1', 3, 1), ('3', 4, 2), ('1', 4, 1), ('1', 5, 1), ('p',), ('3', 6, 2), ('1', 6, 1), ('1', 7, 1), ('3', 8, 2), ('1', 8, 1), ('1', 9, 1), ('1', 10, 1), ('3', 10, 1), ('1', 11, 1), ('3', 11, 1), ('2', 0, 4), ('2', 4, 2), ('2', 6, 2), ('2', 8, 2), ('2', 10, 2), ('g', 0), ('g', 1), ('g', 2)], 'ops': [('C3', 0, 0), ('C3', 1, 4), ('C1', 0, 4), ('C1', 1, 0), ('Q', 0), ('A', 0), ('B', 0), ('Q', 1), ('A', 1), ('B', 1), ('M', 0), ('M', 1), ('H', 0), ('H', 1), ('C3', 2, 0), ('C3', 3, 4), ('C1', 2, 4), ('C1', 3, 0), ('Q', 2), ('A', 2), ('B', 2), ('Q', 3), ('A', 3), ('B', 3), ('M', 2), ('M', 3), ('H', 2), ('H', 3), ('C3', 4, 0), ('C3', 5, 4), ('C1', 4, 4), ('C1', 5, 0), ('Q', 4), ('A', 4), ('B', 4), ('Q', 5), ('A', 5), ('B', 5), ('M', 4), ('M', 5), ('H', 4), ('H', 5), ('C3', 6, 0), ('C3', 7, 4), ('C1', 6, 4), ('C1', 7, 0), ('Q', 6), ('A', 6), ('B', 6), ('Q', 7), ('A', 7), ('B', 7), ('M', 6), ('M', 7), ('H', 6), ('H', 7), ('C3', 8, 0), ('C3', 9, 4), ('C1', 8, 4), ('C1', 9, 0), ('Q', 8), ('A', 8), ('B', 8), ('Q', 9), ('A', 9), ('B', 9), ('M', 8), ('M', 9), ('H', 8), ('H', 9), ('C3', 10, 0), ('C3', 11, 0), ('C1', 10, 4), ('C1', 11, 4), ('Q1', 10), ('A', 10), ('Q3', 10), ('B', 10), ('Q1', 11), ('A', 11), ('Q3', 11), ('B', 11), ('M', 10), ('M', 11), ('H', 10), ('H', 11), ('W', 0, 4, 'VSVV'), ('WQ', 0), ('Y', 0), ('Y', 1), ('Y', 2), ('Y', 3), ('YO', 0, 4, 'S'), ('W', 4, 2, 'SS'), ('WQ', 4), ('Y', 4), ('Y', 5), ('YO', 4, 2, 'S'), ('W', 6, 2, 'VS'), ('WQ', 6), ('Y', 6), ('Y', 7), ('YO', 6, 2, 'S'), ('W', 8, 2, 'VV'), ('WQ', 8), ('Y', 8), ('Y', 9), ('YO', 8, 2, 'S'), ('W', 10, 2, 'SV'), ('WQ', 10), ('Y', 10), ('Y', 11), ('YO', 10, 2, 'S')]}
 GATHERS = ((0, 384), (384, 384), (768, 384), (1152, 384))
 
 
@@ -77,23 +77,19 @@ def tile_moe_tk_glu_gelu_kernel(tc, xT, w1, w3, w2, gate, offs, pos1, pos2, pos3
 
         vcopy, scopy = nc.vector.tensor_copy, nc.scalar.copy
 
-        for e in range(0, E, 2):
-            load(raw3, w3, e, 2)
-            if e in ():
-                load(raw1, w1, e, 1)
-                load(raw1, w1, e + 1, 1)
-            else:
-                load(raw1, w1, e, 2)
-            if e == 4:
+        for item in PLAN["dma"]:
+            kind = item[0]
+            if kind == "p":
                 for tile, source in zip(pos_t, (pos1, pos2, pos3)):
                     nc.sync.dma_start(tile[:], source)
-        for first, count in W2_GROUPS[0:]:
-            load(raw2, w2, first, count)
-        gate_t = []
-        for r in range(3):
-            tile = raws.tile([P, T], F32, name="gate_tile", tag="raw")
-            gate_t.append(tile)
-            nc.sync.dma_start(tile[:], gate[r])
+            elif kind == "g":
+                if item[1] == 0:
+                    gate_t = []
+                tile = raws.tile([P, T], F32, name="gate_tile", tag="raw")
+                gate_t.append(tile)
+                nc.sync.dma_start(tile[:], gate[item[1]])
+            else:
+                load({"1": raw1, "2": raw2, "3": raw3}[kind], {"1": w1, "2": w2, "3": w3}[kind], item[1], item[2])
 
         split = 320
         xb = x_bf[:].rearrange("p t j -> p (t j)")
@@ -190,40 +186,49 @@ def tile_moe_tk_glu_gelu_kernel(tc, xT, w1, w3, w2, gate, offs, pos1, pos2, pos3
             for i in range(src.shape[1] // (4 * N)):
                 q2[first + i] = (codes, scales, i * N)
 
-        def finish(group):
-            first, count = W2_GROUPS[group]
-            engines = ((scopy, vcopy, scopy, vcopy), (scopy, vcopy, scopy, vcopy), (scopy, vcopy), (scopy, vcopy))[group]
-            bf2 = copy_w2(engines, first)
-            quantise_w2(bf2[:], first)
-            for e in range(first, first + count):
-                stage_y(e)
-            y_out(first, count, vcopy if first == 10 else scopy)
+        bf = {}
+        bf2 = {}
 
-        for a in range(0, E, 2):
-            bf = {}
-            for e in (a, a + 1):
+        def get_bf(e):
+            if e not in bf:
                 bf[e] = rounds.tile([P, 8 * H], BF16, align_bytes=64, name="bf")
-            for e, share in ((a, 0), (a + 1, 0)):
-                if share:
-                    interleave_hidden(vcopy, bf[e][:, 4 * H :], raw3[e], 0, share)
-                interleave_hidden(scopy, bf[e][:, 4 * H :], raw3[e], share, 4)
-            for e, share in ((a, 4 if a == E - 2 else 4), (a + 1, 4 if a == E - 2 else 4)):
-                interleave_hidden(vcopy, bf[e][:, : 4 * H], raw1[e], 0, share)
+            return bf[e]
+
+        for op in PLAN["ops"]:
+            k, e = op[0], op[1]
+            if k in ("C1", "C3"):
+                share = op[2]
+                dst = get_bf(e)[:, : 4 * H] if k == "C1" else get_bf(e)[:, 4 * H :]
+                src = (raw1 if k == "C1" else raw3)[e]
+                if share > 0:
+                    interleave_hidden(vcopy, dst, src, 0, share)
                 if share < 4:
-                    interleave_hidden(scopy, bf[e][:, : 4 * H], raw1[e], share, 4)
-            for e in (a, a + 1):
+                    interleave_hidden(scopy, dst, src, share, 4)
+            elif k == "Q":
                 codes, scales = quantise(bf[e][:], "w")
                 q1[e] = (codes, scales, 0)
                 q3[e] = (codes, scales, H)
+            elif k == "Q1":
+                q1[e] = quantise(bf[e][:, : 4 * H], "w1") + (0,)
+            elif k == "Q3":
+                q3[e] = quantise(bf[e][:, 4 * H :], "w3") + (0,)
+            elif k == "A":
                 stage_a(e)
                 stage_gelu(e)
+            elif k == "B":
                 stage_b(e)
-            for e in (a, a + 1):
+            elif k == "M":
                 stage_mult(e)
-            for e in (a, a + 1):
+            elif k == "H":
                 stage_h(e)
-        for group in range(0, len(W2_GROUPS)):
-            finish(group)
+            elif k == "W":
+                bf2[e] = copy_w2([vcopy if c == "V" else scopy for c in op[3]], e)
+            elif k == "WQ":
+                quantise_w2(bf2[e][:], e)
+            elif k == "Y":
+                stage_y(e)
+            elif k == "YO":
+                y_out(e, op[2], vcopy if op[3] == "V" else scopy)
 
         for r in range(2):
             nc.vector.tensor_tensor(prods[:, r, :], y_all[:].indirect(pos_t[r][:]), gate_t[r][:], MULT)

from contextlib import ExitStack

import concourse.mybir as mybir

K, T, E, C, H, N = 512, 512, 12, 128, 512, 128
FLOPS = 2 * E * C * (2 * K * H + H * N)

P = 128
F32 = mybir.dt.float32
BF16 = mybir.dt.bfloat16
U32 = mybir.dt.uint32
U16 = mybir.dt.uint16
U8 = mybir.dt.uint8
FP8X4 = mybir.dt.float8_e4m3fn_x4
MULT = mybir.AluOpType.mult
ADD = mybir.AluOpType.add
GELU = mybir.ActivationFunctionType.Gelu_apprx_tanh

PLAN = {'dma': [('3', 0, 2), ('1', 0, 1), ('1', 1, 1), ('3', 2, 2), ('1', 2, 1), ('1', 3, 1), ('3', 4, 2), ('1', 4, 1), ('1', 5, 1), ('p',), ('3', 6, 2), ('1', 6, 1), ('1', 7, 1), ('3', 8, 2), ('1', 8, 1), ('1', 9, 1), ('1', 10, 1), ('3', 10, 1), ('1', 11, 1), ('3', 11, 1), ('2', 0, 4), ('2', 4, 2), ('2', 6, 2), ('2', 8, 2), ('2', 10, 2), ('g', 0), ('g', 1), ('g', 2)], 'ops': [('C3', 0, 0), ('C3', 1, 4), ('C1', 0, 4), ('C1', 1, 0), ('Q', 0), ('A', 0), ('B', 0), ('Q', 1), ('A', 1), ('B', 1), ('M', 0), ('M', 1), ('H', 0), ('H', 1), ('C3', 2, 0), ('C3', 3, 4), ('C1', 2, 4), ('C1', 3, 0), ('Q', 2), ('A', 2), ('B', 2), ('Q', 3), ('A', 3), ('B', 3), ('M', 2), ('M', 3), ('H', 2), ('H', 3), ('C3', 4, 0), ('C3', 5, 4), ('C1', 4, 4), ('C1', 5, 0), ('Q', 4), ('A', 4), ('B', 4), ('Q', 5), ('A', 5), ('B', 5), ('M', 4), ('M', 5), ('H', 4), ('H', 5), ('C3', 6, 0), ('C3', 7, 4), ('C1', 6, 4), ('C1', 7, 0), ('Q', 6), ('A', 6), ('B', 6), ('Q', 7), ('A', 7), ('B', 7), ('M', 6), ('M', 7), ('H', 6), ('H', 7), ('C3', 8, 0), ('C3', 9, 4), ('C1', 8, 4), ('C1', 9, 0), ('Q', 8), ('A', 8), ('B', 8), ('Q', 9), ('A', 9), ('B', 9), ('M', 8), ('M', 9), ('H', 8), ('H', 9), ('C3', 10, 0), ('C3', 11, 0), ('C1', 10, 4), ('C1', 11, 4), ('Q1', 10), ('A', 10), ('Q3', 10), ('B', 10), ('Q1', 11), ('A', 11), ('Q3', 11), ('B', 11), ('M', 10), ('M', 11), ('H', 10), ('H', 11), ('W', 0, 4, 'VSVV'), ('WQ', 0), ('Y', 0), ('Y', 1), ('Y', 2), ('Y', 3), ('YO', 0, 4, 'S'), ('W', 4, 2, 'SS'), ('WQ', 4), ('Y', 4), ('Y', 5), ('YO', 4, 2, 'S'), ('W', 6, 2, 'VS'), ('WQ', 6), ('Y', 6), ('Y', 7), ('YO', 6, 2, 'S'), ('W', 8, 2, 'VV'), ('WQ', 8), ('Y', 8), ('Y', 9), ('YO', 8, 2, 'S'), ('W', 10, 2, 'SV'), ('WQ', 10), ('Y', 10), ('Y', 11), ('YO', 10, 2, 'S')]}
GATHERS = ((0, 384), (384, 384), (768, 384), (1152, 384))


def tile_moe_tk_glu_gelu_kernel(tc, xT, w1, w3, w2, gate, offs, pos1, pos2, pos3, out):
    nc = tc.nc
    with ExitStack() as ctx:
        keep = ctx.enter_context(tc.tile_pool(name="keep", bufs=1))
        raws = ctx.enter_context(tc.tile_pool(name="raws", bufs=6))
        rounds = ctx.enter_context(tc.tile_pool(name="rounds", bufs=3))
        codes_pool = ctx.enter_context(tc.tile_pool(name="codes", bufs=3))
        h_pool = ctx.enter_context(tc.tile_pool(name="h_codes", bufs=12))
        hidden = ctx.enter_context(tc.tile_pool(name="hidden", bufs=3))
        psum = ctx.enter_context(tc.psum_pool(name="psum", bufs=3))
        psum_y = ctx.enter_context(tc.psum_pool(name="psum_y", bufs=2))

        offs_t = keep.tile([P, E * C // 16], U16, name="offs_t")
        pos_t = [keep.tile([P, T // 16], U16, name=f"pos_t{r}") for r in range(3)]
        x_raw = keep.tile([P, 4, T], F32, name="x_raw")
        x_bf = keep.tile([P, T, 4], BF16, align_bytes=64, name="x_bf")
        x_codes = keep.tile([P, T], U32, align_bytes=64, name="x_codes")
        x_scales = keep.tile([P, T], U8, align_bytes=64, name="x_scales")
        g_codes = keep.tile([P, E * C], U32, align_bytes=64, name="g_codes")
        g_scales = keep.tile([P, E * C], U8, align_bytes=64, name="g_scales")
        y_all = keep.tile([P, E * C], F32, name="y_all")
        prods = keep.tile([P, 3, T], F32, name="prods")
        part = keep.tile([P, T], F32, name="part")
        result = keep.tile([P, T], F32, name="result")
        warm = keep.tile([P, 8], F32, name="warm")

        nc.gpsimd.memset(x_scales[:], 0)
        nc.vector.memset(warm[:], 0.0)
        nc.scalar.activation(warm[:], warm[:], GELU)

        nc.sync.dma_start(x_raw[:], xT.rearrange("(p j) t -> p j t", j=4))
        nc.sync.dma_start(offs_t[:], offs)

        raw1 = {}
        raw3 = {}
        raw2 = {}

        def load(where, source, first, count):
            tile = raws.tile([P, count, 4, source.shape[2]], F32, name="raw", tag="raw")
            nc.sync.dma_start(tile[:], source[first : first + count].rearrange("e (p j) i -> p e j i", j=4))
            for i in range(count):
                where[first + i] = tile[:, i]

        def interleave_hidden(engine_copy, dst, src, t0, t1):
            engine_copy(
                dst.rearrange("p (t m j) -> p m j t", t=4, j=4)[:, :, :, t0:t1],
                src.rearrange("p j (m t) -> p m j t", t=4)[:, :, :, t0:t1],
            )

        def interleave(engine_copy, dst, src):
            engine_copy(
                dst.rearrange("p (c i j) -> p c j i", i=4, j=4),
                src.rearrange("p j (c i) -> p c j i", i=4),
            )

        vcopy, scopy = nc.vector.tensor_copy, nc.scalar.copy

        for item in PLAN["dma"]:
            kind = item[0]
            if kind == "p":
                for tile, source in zip(pos_t, (pos1, pos2, pos3)):
                    nc.sync.dma_start(tile[:], source)
            elif kind == "g":
                if item[1] == 0:
                    gate_t = []
                tile = raws.tile([P, T], F32, name="gate_tile", tag="raw")
                gate_t.append(tile)
                nc.sync.dma_start(tile[:], gate[item[1]])
            else:
                load({"1": raw1, "2": raw2, "3": raw3}[kind], {"1": w1, "2": w2, "3": w3}[kind], item[1], item[2])

        split = 320
        xb = x_bf[:].rearrange("p t j -> p (t j)")
        interleave(vcopy, xb[:, : 4 * split], x_raw[:, :, :split])
        interleave(scopy, xb[:, 4 * split :], x_raw[:, :, split:])
        nc.vector.quantize_mx(out=x_codes[:].bitcast(FP8X4), scales=x_scales[:], in_=xb)
        for s, n in GATHERS:
            lists = offs_t[:, s // 16 : (s + n) // 16]
            nc.vector.tensor_copy(g_codes[:, s : s + n], x_codes[:].indirect(lists))
            nc.vector.tensor_copy(g_scales[:, s : s + n], x_scales[:].indirect(lists))

        q1 = {}
        q3 = {}
        q2 = {}
        qh = {}
        acc_a = {}
        acc_b = {}
        act = {}
        hb = {}
        y_banks = {}

        def quantise(src, tag, pool=codes_pool):
            width = src.shape[1] // 4
            codes = pool.tile([P, width], U32, align_bytes=64, name=f"codes_{tag}")
            scales = pool.tile([P, width], U8, align_bytes=64, name=f"scales_{tag}")
            nc.vector.quantize_mx(out=codes[:].bitcast(FP8X4), scales=scales[:], in_=src)
            return codes, scales

        def product(bank, q, e):
            codes, scales, at = q
            for t in range(4):
                cols = slice(at + t * P, at + (t + 1) * P)
                nc.tensor.matmul_mx(
                    out=bank[:, t, :],
                    lhsT=codes[:, cols].bitcast(FP8X4),
                    lhsT_scale=scales[:, cols],
                    rhs=g_codes[:, e * C : (e + 1) * C].bitcast(FP8X4),
                    rhs_scale=g_scales[:, e * C : (e + 1) * C],
                    start=True,
                    stop=True,
                )

        def stage_a(e):
            acc_a[e] = psum.tile([P, 4, C], F32, name="acc_a")
            product(acc_a[e], q1[e], e)

        def stage_b(e):
            acc_b[e] = psum.tile([P, 4, C], F32, name="acc_b")
            product(acc_b[e], q3[e], e)

        def stage_gelu(e):
            act[e] = hidden.tile([P, C, 4], F32, name="act")
            nc.scalar.activation(act[e][:], acc_a[e][:].rearrange("p t n -> p n t"), GELU)

        def stage_mult(e):
            hb[e] = hidden.tile([P, C * 4], BF16, align_bytes=64, name="hb")
            nc.vector.tensor_tensor(
                hb[e][:].rearrange("p (n t) -> p n t", t=4), act[e][:], acc_b[e][:].rearrange("p t n -> p n t"), MULT
            )

        def stage_h(e):
            qh[e] = quantise(hb[e][:], "h", h_pool)

        def stage_y(e):
            h_codes, h_scales = qh[e]
            g = e // 4
            if e % 4 == 0:
                y_banks[g] = psum_y.tile([P, 4, C], F32, name="y_bank")
            codes, scales, at = q2[e]
            nc.tensor.matmul_mx(
                out=y_banks[g][:, e % 4, :],
                lhsT=codes[:, at : at + N].bitcast(FP8X4),
                lhsT_scale=scales[:, at : at + N],
                rhs=h_codes[:].bitcast(FP8X4),
                rhs_scale=h_scales[:],
                start=True,
                stop=True,
            )

        def y_out(first, count, copy):
            copy(
                y_all[:, first * C : (first + count) * C],
                y_banks[first // 4][:, first % 4 : first % 4 + count, :].rearrange("p e n -> p (e n)"),
            )

        def copy_w2(engines, first):
            bf = rounds.tile([P, len(engines) * 4 * N], BF16, align_bytes=64, name="bf2")
            for i, engine in enumerate(engines):
                interleave(engine, bf[:, i * 4 * N : (i + 1) * 4 * N], raw2[first + i])
            return bf

        def quantise_w2(src, first):
            codes, scales = quantise(src, "w2")
            for i in range(src.shape[1] // (4 * N)):
                q2[first + i] = (codes, scales, i * N)

        bf = {}
        bf2 = {}

        def get_bf(e):
            if e not in bf:
                bf[e] = rounds.tile([P, 8 * H], BF16, align_bytes=64, name="bf")
            return bf[e]

        for op in PLAN["ops"]:
            k, e = op[0], op[1]
            if k in ("C1", "C3"):
                share = op[2]
                dst = get_bf(e)[:, : 4 * H] if k == "C1" else get_bf(e)[:, 4 * H :]
                src = (raw1 if k == "C1" else raw3)[e]
                if share > 0:
                    interleave_hidden(vcopy, dst, src, 0, share)
                if share < 4:
                    interleave_hidden(scopy, dst, src, share, 4)
            elif k == "Q":
                codes, scales = quantise(bf[e][:], "w")
                q1[e] = (codes, scales, 0)
                q3[e] = (codes, scales, H)
            elif k == "Q1":
                q1[e] = quantise(bf[e][:, : 4 * H], "w1") + (0,)
            elif k == "Q3":
                q3[e] = quantise(bf[e][:, 4 * H :], "w3") + (0,)
            elif k == "A":
                stage_a(e)
                stage_gelu(e)
            elif k == "B":
                stage_b(e)
            elif k == "M":
                stage_mult(e)
            elif k == "H":
                stage_h(e)
            elif k == "W":
                bf2[e] = copy_w2([vcopy if c == "V" else scopy for c in op[3]], e)
            elif k == "WQ":
                quantise_w2(bf2[e][:], e)
            elif k == "Y":
                stage_y(e)
            elif k == "YO":
                y_out(e, op[2], vcopy if op[3] == "V" else scopy)

        for r in range(2):
            nc.vector.tensor_tensor(prods[:, r, :], y_all[:].indirect(pos_t[r][:]), gate_t[r][:], MULT)
        halves = ((0, 256), (256, 256))
        for i, (s, n) in enumerate(halves):
            nc.vector.tensor_tensor(
                prods[:, 2, s : s + n], y_all[:].indirect(pos_t[2][:, s // 16 : (s + n) // 16]), gate_t[2][:, s : s + n], MULT
            )
            if i == 0:
                nc.vector.tensor_tensor(part[:], prods[:, 0, :], prods[:, 1, :], ADD)
            nc.vector.tensor_tensor(result[:, s : s + n], part[:, s : s + n], prods[:, 2, s : s + n], ADD)
            nc.sync.dma_start(out[:, s : s + n], result[:, s : s + n])
